import numpy as np
import ml_dtypes


def mxq(x, axis, fmt="e4m3"):
    dtype, down = {"e4m3": (ml_dtypes.float8_e4m3fn, 7), "e5m2": (ml_dtypes.float8_e5m2, 14)}[fmt]
    v = np.moveaxis(np.asarray(x, np.float32).astype(ml_dtypes.bfloat16).astype(np.float64), axis, -1)
    blocks = v.reshape(v.shape[:-1] + (-1, 32))
    amax = np.abs(blocks).max(-1, keepdims=True)
    byte = np.maximum(np.where(amax > 0, np.frexp(amax)[1] - 1 + 127, 0) - down, 1)
    scale = np.exp2(byte - 127.0)
    codes = (blocks / scale).astype(np.float32).astype(dtype).astype(np.float64)
    return np.moveaxis((codes * scale).reshape(v.shape), -1, axis)


WIDE = False


def mx_kscale(k):
    if not WIDE:
        return np.ones(k)
    levels = np.array([24, -24, 12, -12, 0])
    if k % 512:
        return np.exp2(np.random.permutation(np.resize(levels, k // 32))).repeat(32)
    a = np.empty((k // 512, 16))
    for p in range(k // 512):
        a[p, :8] = np.random.permutation(np.resize(levels, 8))
        for g in range(8):
            far = levels[np.abs(levels - a[p, g]) >= 10]
            a[p, g + 8] = far[np.random.randint(len(far))]
    return np.exp2(a.ravel()).repeat(32)


def f64(x):
    return np.asarray(x).astype(np.float64)


def striped(idx):
    return np.tile(idx.reshape(-1, 16).T, (8, 1)).astype(np.uint16)


def unstriped(offs):
    return offs[:16].T.reshape(-1).astype(np.int64)


E2M1 = np.array([0.0, 0.5, 1.0, 1.5, 2.0, 3.0, 4.0, 6.0, -0.0, -0.5, -1.0, -1.5, -2.0, -3.0, -4.0, -6.0])


def pack_weight(w, fmt):
    k, n = w.shape
    w = f64(np.asarray(w, np.float32).astype(ml_dtypes.bfloat16)).reshape(k // 32, 32, n)
    amax = np.abs(w).max(1)
    if fmt == "e4m3":
        byte = np.frexp(amax)[1] - 1 + 127 - 7
    else:
        mant, ex = np.frexp(amax / 6.0)
        byte = np.where(mant > 0.5, ex, ex - 1) + 127
    byte = np.clip(np.where(amax > 0, byte, 1), 1, 254)
    scaled = (w * np.exp2(127.0 - byte)[:, None, :]).reshape(k, n).astype(np.float32)
    by_word = np.ascontiguousarray(scaled.reshape(k // 512, 128, 4, n).transpose(0, 1, 3, 2))
    if fmt == "e4m3":
        words = by_word.astype(ml_dtypes.float8_e4m3fn).view(np.uint8)
    else:
        c = by_word.astype(ml_dtypes.float4_e2m1fn).view(np.uint8) & 0xF
        words = (c[..., 0::2] | (c[..., 1::2] << 4)).reshape(k // 512, 128, 2 * n)
    return np.ascontiguousarray(words), np.ascontiguousarray(byte.astype(np.uint8).reshape(k // 512, 16, n))


def unpack_weight(words, scales, fmt):
    g, _, n = scales.shape
    words = np.ascontiguousarray(words).reshape(g, 128, n, -1)
    if fmt == "e4m3":
        vals = words.view(ml_dtypes.float8_e4m3fn).astype(np.float64)
    else:
        nib = np.empty((g, 128, n, 4), np.uint8)
        nib[..., 0::2] = words & 0xF
        nib[..., 1::2] = words >> 4
        vals = E2M1[nib]
    vals = vals * np.repeat(np.exp2(scales.astype(np.float64) - 127.0), 8, axis=1)[..., None]
    return vals.transpose(0, 1, 3, 2).reshape(g * 512, n)


K, R, N, T, J = 512, 1024, 256, 1024, 512


def setup_inputs():
    n = np.random.standard_normal
    s = mx_kscale(K)[:, None]
    u = mx_kscale(R)[:, None]
    wd = n((R, N)) / np.sqrt(R) / u
    p_tab = pack_weight(n((K, T)) * s, "e4m3")
    p_wg = pack_weight(n((K, R)) / np.sqrt(K) / s, "e2m1")
    p_wu = pack_weight(n((K, R)) / np.sqrt(K) / s * u.T, "e2m1")
    p_wd8 = pack_weight(wd[:512], "e4m3")
    p_wd4 = pack_weight(wd[512:], "e2m1")
    return {
        "tab_words": p_tab[0],
        "tab_scales": p_tab[1],
        "wg_words": p_wg[0],
        "wg_scales": p_wg[1],
        "wu_words": p_wu[0],
        "wu_scales": p_wu[1],
        "wd8_words": p_wd8[0],
        "wd8_scales": p_wd8[1],
        "wd4_words": p_wd4[0],
        "wd4_scales": p_wd4[1],
        "offs": striped(np.random.permutation(T)[:J]),
    }


def reference(tab_words, tab_scales, wg_words, wg_scales, wu_words, wu_scales, wd8_words, wd8_scales, wd4_words, wd4_scales, offs):
    idx = unstriped(offs)
    tab_ = unpack_weight(tab_words, tab_scales, "e4m3")[:, idx]
    wg_ = unpack_weight(wg_words, wg_scales, "e2m1")
    wu_ = unpack_weight(wu_words, wu_scales, "e2m1")
    ga = wg_.T @ tab_
    ub = wu_.T @ tab_
    h = np.maximum(ga, 0.0) * ub
    h_ = mxq(h, 0, "e4m3")
    wd8_ = unpack_weight(wd8_words, wd8_scales, "e4m3")
    wd4_ = unpack_weight(wd4_words, wd4_scales, "e2m1")
    y = wd8_.T @ h_[:512] + wd4_.T @ h_[512:]
    return y

@@ -1,0 +1,227 @@
+from contextlib import ExitStack
+
+import concourse.mybir as mybir
+from concourse.masks import make_identity
+
+K, R, N, T, J = 512, 1024, 256, 1024, 512
+FLOPS = 2 * K * R * J * 2 + 2 * R * N * J
+
+F32 = mybir.dt.float32
+BF16 = mybir.dt.bfloat16
+I32 = mybir.dt.int32
+U32 = mybir.dt.uint32
+U16 = mybir.dt.uint16
+U8 = mybir.dt.uint8
+FP8X4 = mybir.dt.float8_e4m3fn_x4
+FP4X4 = mybir.dt.float4_e2m1fn_x4
+RELU = mybir.ActivationFunctionType.Relu
+MULT = mybir.AluOpType.mult
+
+P = 128
+TOK = 128
+TILES = J // TOK
+PASS = 512
+HALVES = R // PASS
+
+
+def tile_list_gmlpt_relu_mix_none_kernel(
+    tc, tab_words, tab_scales, wg_words, wg_scales, wu_words, wu_scales,
+    wd8_words, wd8_scales, wd4_words, wd4_scales, offs, out,
+):
+    nc = tc.nc
+    with ExitStack() as ctx:
+        keep = ctx.enter_context(tc.tile_pool(name="keep", bufs=1))
+        ring = ctx.enter_context(tc.tile_pool(name="ring", bufs=2))
+        psum = ctx.enter_context(tc.psum_pool(name="psum", bufs=2))
+
+        def plane(name, width):
+            tile = keep.tile([P, width // 4], I32, name=name, align_bytes=64)
+            nc.vector.memset(tile[:], 0)
+            return tile
+
+        def load_rows(tile, scales, q):
+            nc.sync.dma_start(tile[32 * q : 32 * q + 4, :], scales[0, 4 * q : 4 * q + 4, :].bitcast(I32))
+
+        offsets = keep.tile([P, J // 16], U16, name="offsets")
+        nc.sync.dma_start(offsets[:], offs)
+        wg_w = keep.tile([P, 2 * R], U8, name="wg_w", align_bytes=64)
+        nc.gpsimd.dma_start(wg_w[:].bitcast(I32), wg_words[0].bitcast(I32))
+        wu_w = keep.tile([P, 2 * R], U8, name="wu_w", align_bytes=64)
+        nc.gpsimd.dma_start(wu_w[:].bitcast(I32), wu_words[0].bitcast(I32))
+
+        tab_s = plane("tab_s", T)
+        wg_s = plane("wg_s", R)
+        ident = keep.tile([P, P], F32, name="ident", align_bytes=64)
+        nc.vector.memset(ident[:], 0.0)
+        wu_s = plane("wu_s", R)
+        for q in range(4):
+            load_rows(tab_s, tab_scales, q)
+        load_rows(wg_s, wg_scales, 0)
+        tab_w = keep.tile([P, T], I32, name="tab_w", align_bytes=64)
+        nc.sync.dma_start(tab_w[:], tab_words[0].rearrange("p t i -> p (t i)").bitcast(I32))
+        for q in range(1, 4):
+            load_rows(wg_s, wg_scales, q)
+        for q in range(4):
+            load_rows(wu_s, wu_scales, q)
+
+        warm_pe = psum.tile([P, 4, P], F32, name="warm_pe", tag="y")
+        for i in range(24):
+            nc.tensor.transpose(warm_pe[:, i % 4, :], ident[:], ident[:])
+        wd8_w = keep.tile([P, N], I32, name="wd8_w", align_bytes=64)
+        nc.gpsimd.dma_start(wd8_w[:], wd8_words[0].rearrange("p n i -> p (n i)").bitcast(I32))
+        wd4_w = keep.tile([P, 2 * N], U8, name="wd4_w", align_bytes=64)
+        nc.gpsimd.dma_start(wd4_w[:].bitcast(I32), wd4_words[0].bitcast(I32))
+        make_identity(nc, ident[:], nomemset=True)
+        wd8_s = plane("wd8_s", N)
+        wd4_s = plane("wd4_s", N)
+        for q in range(4):
+            load_rows(wd8_s, wd8_scales, q)
+        for q in range(4):
+            load_rows(wd4_s, wd4_scales, q)
+
+        v_w, v_s, gate, up, relu, h, ht, hq, codes, cscales, y = ({} for i in range(11))
+
+        def gather(t):
+            cols = offsets[:, t * TOK // 16 : (t + 1) * TOK // 16]
+            v_w[t] = keep.tile([P, TOK], U32, name="v_w%d" % t, align_bytes=64)
+            v_s[t] = keep.tile([P, TOK], U8, name="v_s%d" % t, align_bytes=64)
+            nc.vector.tensor_copy(v_w[t][:], tab_w[:].bitcast(U32).indirect(cols))
+            nc.vector.tensor_copy(v_s[t][:], tab_s[:].bitcast(U8).indirect(cols))
+
+        def product(t, b, words, scales, tag):
+            acc = psum.tile([P, PASS], F32, name=tag, tag=tag)
+            nc.tensor.matmul_mx(
+                out=acc[:],
+                lhsT=v_w[t][:].bitcast(FP8X4),
+                lhsT_scale=v_s[t][:],
+                rhs=words[:, 2 * PASS * b : 2 * PASS * (b + 1)].bitcast(FP4X4),
+                rhs_scale=scales[:].bitcast(U8)[:, PASS * b : PASS * (b + 1)],
+                start=True,
+                stop=True,
+            )
+            return acc
+
+        def first_layer(t, b):
+            gate[t, b] = product(t, b, wg_w, wg_s, "gate")
+            up[t, b] = product(t, b, wu_w, wu_s, "up")
+
+        def rectify(t, b):
+            relu[t, b] = ring.tile([P, 2, P, 2], F32, name="relu", tag="relu", bufs=3)
+            nc.scalar.activation(relu[t, b][:], gate[t, b][:].rearrange("j (p u e) -> j u p e", u=2, e=2), RELU)
+
+        def multiply(t, b):
+            h[t, b] = keep.tile([P, 2, P, 2], BF16, name="h%d_%d" % (t, b), align_bytes=64)
+            nc.vector.tensor_tensor(h[t, b][:], up[t, b][:].rearrange("j (p u e) -> j u p e", u=2, e=2), relu[t, b][:], MULT)
+
+        def turn(t, bs):
+            acc = psum.tile([P, len(bs), 2, TOK], F32, name="ht", tag="ht")
+            for i, b in enumerate(bs):
+                words = h[t, b][:].rearrange("j u p e -> j (u p e)").bitcast(F32)
+                for u in range(2):
+                    nc.tensor.transpose(acc[:, i, u, :], words[:, P * u : P * (u + 1)], ident[:])
+            ht[t, bs] = acc
+
+        def interleave(t, bs):
+            tile = keep.tile([P, len(bs), TOK, 2], F32, name="hq%d_%d" % (t, bs[0]), align_bytes=64)
+            nc.scalar.copy(tile[:], ht[t, bs][:].rearrange("p b u j -> p b j u"))
+            hq[t, bs] = tile
+
+        def quantise(t, bs):
+            c = keep.tile([P, len(bs) * TOK], U32, name="codes%d_%d" % (t, bs[0]), align_bytes=64)
+            s = keep.tile([P, len(bs) * TOK], U8, name="cscales%d_%d" % (t, bs[0]), align_bytes=64)
+            nc.vector.quantize_mx(
+                out=c[:].bitcast(FP8X4),
+                scales=s[:],
+                in_=hq[t, bs][:].rearrange("p b j u -> p (b j u)").bitcast(BF16),
+            )
+            for i, b in enumerate(bs):
+                codes[t, b] = c[:, TOK * i : TOK * (i + 1)]
+                cscales[t, b] = s[:, TOK * i : TOK * (i + 1)]
+
+        def down_pass(acc, t, b, half):
+            n0 = P * half
+            if b == 0:
+                lhs = wd8_w[:, n0 : n0 + P].bitcast(FP8X4)
+                lhs_s = wd8_s[:].bitcast(U8)[:, n0 : n0 + P]
+            else:
+                lhs = wd4_w[:, 2 * n0 : 2 * (n0 + P)].bitcast(FP4X4)
+                lhs_s = wd4_s[:].bitcast(U8)[:, n0 : n0 + P]
+            nc.tensor.matmul_mx(
+                out=acc, lhsT=lhs, lhsT_scale=lhs_s,
+                rhs=codes[t, b].bitcast(FP8X4), rhs_scale=cscales[t, b],
+                start=(b == 0), stop=(b == 1),
+            )
+
+        out_v = out.rearrange("(h p) j -> p h j", p=P)
+
+        def second_layer(t):
+            y[t] = psum.tile([P, 2, TOK], F32, name="y", tag="y")
+            for half in range(2):
+                for b in range(HALVES):
+                    down_pass(y[t][:, half, :], t, b, half)
+
+        def store(t, engine_copy):
+            res = keep.tile([P, 2, TOK], F32, name="res%d" % t)
+            engine_copy(res[:], y[t][:])
+            nc.sync.dma_start(out_v[:, :, TOK * t : TOK * (t + 1)], res[:])
+
+        both = (0, 1)
+        last = TILES - 1
+        gather(0)
+        first_layer(0, 0)
+        gather(1)
+        rectify(0, 0)
+        first_layer(0, 1)
+        gather(2)
+        multiply(0, 0)
+        rectify(0, 1)
+        first_layer(1, 0)
+        gather(3)
+        multiply(0, 1)
+        rectify(1, 0)
+        first_layer(1, 1)
+        turn(0, both)
+        multiply(1, 0)
+        rectify(1, 1)
+        first_layer(2, 0)
+        interleave(0, both)
+        multiply(1, 1)
+        rectify(2, 0)
+        first_layer(2, 1)
+        turn(1, both)
+        quantise(0, both)
+        multiply(2, 0)
+        rectify(2, 1)
+        first_layer(3, 0)
+        second_layer(0)
+        interleave(1, both)
+        multiply(2, 1)
+        rectify(3, 0)
+        first_layer(3, 1)
+        turn(2, both)
+        store(0, nc.vector.tensor_copy)
+        quantise(1, both)
+        multiply(3, 0)
+        rectify(3, 1)
+        second_layer(1)
+        turn(last, (0,))
+        interleave(2, both)
+        multiply(3, 1)
+        turn(last, (1,))
+        interleave(last, (0,))
+        quantise(2, both)
+        store(1, nc.vector.tensor_copy)
+        second_layer(2)
+        interleave(last, (1,))
+        quantise(last, (0,))
+        store(2, nc.scalar.copy)
+        quantise(last, (1,))
+        ya = psum.tile([P, TOK], F32, name="ya", tag="gate")
+        yb = psum.tile([P, TOK], F32, name="yb", tag="up")
+        for b in range(HALVES):
+            down_pass(ya[:], last, b, 0)
+            down_pass(yb[:], last, b, 1)
+        res = keep.tile([P, 2, TOK], F32, name="res_last")
+        nc.vector.tensor_copy(res[:, 0, :], ya[:])
+        nc.scalar.copy(res[:, 1, :], yb[:])
+        nc.sync.dma_start(out_v[:, :, TOK * last : TOK * (last + 1)], res[:])

@@ -50,22 +50,24 @@ def tile_list_gmlpt_relu_mix_none_kernel(
         nc.gpsimd.dma_start(wu_w[:].bitcast(I32), wu_words[0].bitcast(I32))
 
         tab_s = plane("tab_s", T)
-        wg_s = plane("wg_s", R)
         ident = keep.tile([P, P], F32, name="ident", align_bytes=64)
         nc.vector.memset(ident[:], 0.0)
         wu_s = plane("wu_s", R)
+        wg_s = plane("wg_s", R)
         for q in range(4):
             load_rows(tab_s, tab_scales, q)
-        load_rows(wg_s, wg_scales, 0)
+        load_rows(wu_s, wu_scales, 0)
         tab_w = keep.tile([P, T], I32, name="tab_w", align_bytes=64)
         nc.sync.dma_start(tab_w[:], tab_words[0].rearrange("p t i -> p (t i)").bitcast(I32))
-        for q in range(1, 4):
+        load_rows(wu_s, wu_scales, 1)
+        for q in range(3):
             load_rows(wg_s, wg_scales, q)
-        for q in range(4):
-            load_rows(wu_s, wu_scales, q)
+        load_rows(wu_s, wu_scales, 2)
+        load_rows(wg_s, wg_scales, 3)
+        load_rows(wu_s, wu_scales, 3)
 
         warm_pe = psum.tile([P, 4, P], F32, name="warm_pe", tag="y")
-        for i in range(24):
+        for i in range(22):
             nc.tensor.transpose(warm_pe[:, i % 4, :], ident[:], ident[:])
         wd8_w = keep.tile([P, N], I32, name="wd8_w", align_bytes=64)
         nc.gpsimd.dma_start(wd8_w[:], wd8_words[0].rearrange("p n i -> p (n i)").bitcast(I32))
@@ -221,7 +223,9 @@ def tile_list_gmlpt_relu_mix_none_kernel(
         for b in range(HALVES):
             down_pass(ya[:], last, b, 0)
             down_pass(yb[:], last, b, 1)
-        res = keep.tile([P, 2, TOK], F32, name="res_last")
-        nc.vector.tensor_copy(res[:, 0, :], ya[:])
-        nc.scalar.copy(res[:, 1, :], yb[:])
-        nc.sync.dma_start(out_v[:, :, TOK * last : TOK * (last + 1)], res[:])
+        res_a = keep.tile([P, TOK], F32, name="res_a")
+        res_b = keep.tile([P, TOK], F32, name="res_b")
+        nc.vector.tensor_copy(res_a[:], ya[:])
+        nc.sync.dma_start(out_v[:, 0, TOK * last : TOK * (last + 1)], res_a[:])
+        nc.scalar.copy(res_b[:], yb[:])
+        nc.scalar.dma_start(out_v[:, 1, TOK * last : TOK * (last + 1)], res_b[:])

@@ -32,7 +32,7 @@ def tile_list_gmlpt_relu_mix_none_kernel(
     with ExitStack() as ctx:
         keep = ctx.enter_context(tc.tile_pool(name="keep", bufs=1))
         ring = ctx.enter_context(tc.tile_pool(name="ring", bufs=2))
-        psum = ctx.enter_context(tc.psum_pool(name="psum", bufs=2))
+        psum = ctx.enter_context(tc.psum_pool(name="psum", bufs=8))
 
         def plane(name, width):
             tile = keep.tile([P, width // 4], I32, name=name, align_bytes=64)
@@ -45,98 +45,139 @@ def tile_list_gmlpt_relu_mix_none_kernel(
         offsets = keep.tile([P, J // 16], U16, name="offsets")
         nc.sync.dma_start(offsets[:], offs)
         wg_w = keep.tile([P, 2 * R], U8, name="wg_w", align_bytes=64)
-        nc.gpsimd.dma_start(wg_w[:].bitcast(I32), wg_words[0].bitcast(I32))
-        wu_w = keep.tile([P, 2 * R], U8, name="wu_w", align_bytes=64)
-        nc.gpsimd.dma_start(wu_w[:].bitcast(I32), wu_words[0].bitcast(I32))
+        nc.sync.dma_start(wg_w[:].bitcast(I32), wg_words[0].bitcast(I32))
+        wu_lo = keep.tile([P, 2 * PASS], U8, name="wu_lo", align_bytes=64)
+        nc.gpsimd.dma_start(wu_lo[:].bitcast(I32), wu_words[0, :, 0 : 2 * PASS].bitcast(I32))
 
         tab_s = plane("tab_s", T)
+        wu_s = plane("wu_s", R)
         ident = keep.tile([P, P], F32, name="ident", align_bytes=64)
         nc.vector.memset(ident[:], 0.0)
-        wu_s = plane("wu_s", R)
         wg_s = plane("wg_s", R)
+        wd8_s = plane("wd8_s", N)
+        wd4_s = plane("wd4_s", N)
         for q in range(4):
             load_rows(tab_s, tab_scales, q)
         load_rows(wu_s, wu_scales, 0)
         tab_w = keep.tile([P, T], I32, name="tab_w", align_bytes=64)
         nc.sync.dma_start(tab_w[:], tab_words[0].rearrange("p t i -> p (t i)").bitcast(I32))
         load_rows(wu_s, wu_scales, 1)
-        for q in range(3):
-            load_rows(wg_s, wg_scales, q)
         load_rows(wu_s, wu_scales, 2)
-        load_rows(wg_s, wg_scales, 3)
+        for q in range(4):
+            load_rows(wg_s, wg_scales, q)
         load_rows(wu_s, wu_scales, 3)
+        wu_hi = keep.tile([P, 2 * PASS], U8, name="wu_hi", align_bytes=64)
+        nc.sync.dma_start(wu_hi[:].bitcast(I32), wu_words[0, :, 2 * PASS : 4 * PASS].bitcast(I32))
 
-        warm_pe = psum.tile([P, 4, P], F32, name="warm_pe", tag="y")
-        for i in range(22):
+        warm_pe = psum.tile([P, 4, P], F32, name="warm_pe", tag="bank")
+        for i in range(24):
             nc.tensor.transpose(warm_pe[:, i % 4, :], ident[:], ident[:])
+        make_identity(nc, ident[:], nomemset=True)
         wd8_w = keep.tile([P, N], I32, name="wd8_w", align_bytes=64)
         nc.gpsimd.dma_start(wd8_w[:], wd8_words[0].rearrange("p n i -> p (n i)").bitcast(I32))
         wd4_w = keep.tile([P, 2 * N], U8, name="wd4_w", align_bytes=64)
         nc.gpsimd.dma_start(wd4_w[:].bitcast(I32), wd4_words[0].bitcast(I32))
-        make_identity(nc, ident[:], nomemset=True)
-        wd8_s = plane("wd8_s", N)
-        wd4_s = plane("wd4_s", N)
         for q in range(4):
             load_rows(wd8_s, wd8_scales, q)
         for q in range(4):
             load_rows(wd4_s, wd4_scales, q)
 
-        v_w, v_s, gate, up, relu, h, ht, hq, codes, cscales, y = ({} for i in range(11))
+        v_w, v_s, gate, up, relu, h, ht, hq, codes, cscales = ({} for i in range(10))
 
-        def gather(t):
-            cols = offsets[:, t * TOK // 16 : (t + 1) * TOK // 16]
-            v_w[t] = keep.tile([P, TOK], U32, name="v_w%d" % t, align_bytes=64)
+        def gather_scales(t):
             v_s[t] = keep.tile([P, TOK], U8, name="v_s%d" % t, align_bytes=64)
-            nc.vector.tensor_copy(v_w[t][:], tab_w[:].bitcast(U32).indirect(cols))
-            nc.vector.tensor_copy(v_s[t][:], tab_s[:].bitcast(U8).indirect(cols))
+            nc.vector.tensor_copy(v_s[t][:], tab_s[:].bitcast(U8).indirect(offsets[:, t * TOK // 16 : (t + 1) * TOK // 16]))
 
-        def product(t, b, words, scales, tag):
-            acc = psum.tile([P, PASS], F32, name=tag, tag=tag)
+        def gather_words(t):
+            v_w[t] = keep.tile([P, TOK], U32, name="v_w%d" % t, align_bytes=64)
+            nc.vector.tensor_copy(v_w[t][:], tab_w[:].bitcast(U32).indirect(offsets[:, t * TOK // 16 : (t + 1) * TOK // 16]))
+
+        def part_words(name, words):
+            tile = keep.tile([P, 2 * PASS], U8, name=name, align_bytes=64)
+            nc.vector.tensor_copy(
+                tile[:].bitcast(U16).rearrange("p (i c m) -> p c i m", i=4, m=8),
+                words.bitcast(U16).rearrange("p (c m i) -> p c i m", i=4, m=8),
+            )
+            return tile
+
+        def part_scales(name, scales):
+            tile = keep.tile([P, PASS], U8, name=name, align_bytes=64)
+            nc.vector.tensor_copy(
+                tile[:].rearrange("p (i c m) -> p c i m", i=4, m=16),
+                scales[:].bitcast(U8)[:, PASS : 2 * PASS].rearrange("p (c m i) -> p c i m", i=4, m=16),
+            )
+            return tile
+
+        def product_lo(t, words, scales):
+            acc = psum.tile([P, PASS], F32, name="acc", tag="bank")
             nc.tensor.matmul_mx(
                 out=acc[:],
                 lhsT=v_w[t][:].bitcast(FP8X4),
                 lhsT_scale=v_s[t][:],
-                rhs=words[:, 2 * PASS * b : 2 * PASS * (b + 1)].bitcast(FP4X4),
-                rhs_scale=scales[:].bitcast(U8)[:, PASS * b : PASS * (b + 1)],
+                rhs=words.bitcast(FP4X4),
+                rhs_scale=scales[:].bitcast(U8)[:, 0:PASS],
                 start=True,
                 stop=True,
             )
-            return acc
+            return acc[:].rearrange("j (p u e) -> j u p e", u=2, e=2)
 
-        def first_layer(t, b):
-            gate[t, b] = product(t, b, wg_w, wg_s, "gate")
-            up[t, b] = product(t, b, wu_w, wu_s, "up")
+        def product_hi(t, words, scales):
+            acc = psum.tile([P, 4, TOK], F32, name="acc", tag="bank")
+            for i in range(4):
+                nc.tensor.matmul_mx(
+                    out=acc[:, i, :],
+                    lhsT=words[:, 2 * P * i : 2 * P * (i + 1)].bitcast(FP4X4),
+                    lhsT_scale=scales[:, P * i : P * (i + 1)],
+                    rhs=v_w[t][:].bitcast(FP8X4),
+                    rhs_scale=v_s[t][:],
+                    start=True,
+                    stop=True,
+                )
+            return acc[:].rearrange("p i j -> p j i")
+
+        def gate_product(t, b):
+            gate[t, b] = product_hi(t, wg_hi_w, wg_hi_s) if b else product_lo(t, wg_w[:, 0 : 2 * PASS], wg_s)
+
+        def up_product(t, b):
+            up[t, b] = product_hi(t, wu_hi_w, wu_hi_s) if b else product_lo(t, wu_lo[:], wu_s)
 
         def rectify(t, b):
-            relu[t, b] = ring.tile([P, 2, P, 2], F32, name="relu", tag="relu", bufs=3)
-            nc.scalar.activation(relu[t, b][:], gate[t, b][:].rearrange("j (p u e) -> j u p e", u=2, e=2), RELU)
+            relu[t, b] = keep.tile([P, TOK, 4] if b else [P, 2, P, 2], F32, name="relu%d_%d" % (t, b))
+            nc.scalar.activation(relu[t, b][:], gate[t, b], RELU)
 
         def multiply(t, b):
-            h[t, b] = keep.tile([P, 2, P, 2], BF16, name="h%d_%d" % (t, b), align_bytes=64)
-            nc.vector.tensor_tensor(h[t, b][:], up[t, b][:].rearrange("j (p u e) -> j u p e", u=2, e=2), relu[t, b][:], MULT)
+            if b:
+                ts = GROUP[t]
+                if (ts, b) not in hq:
+                    hq[ts, b] = keep.tile([P, len(ts), TOK, 2], F32, name="hq%d_1" % t, align_bytes=64)
+                dst = hq[ts, b][:, ts.index(t)].bitcast(BF16)
+            else:
+                h[t, b] = keep.tile([P, 2, P, 2], BF16, name="h%d_%d" % (t, b), align_bytes=64)
+                dst = h[t, b][:]
+            nc.vector.tensor_tensor(dst, up[t, b], relu[t, b][:], MULT)
 
-        def turn(t, bs):
-            acc = psum.tile([P, len(bs), 2, TOK], F32, name="ht", tag="ht")
-            for i, b in enumerate(bs):
+        def turn(ts, b):
+            acc = psum.tile([P, len(ts), 2, TOK], F32, name="ht", tag="bank")
+            for i, t in enumerate(ts):
                 words = h[t, b][:].rearrange("j u p e -> j (u p e)").bitcast(F32)
                 for u in range(2):
                     nc.tensor.transpose(acc[:, i, u, :], words[:, P * u : P * (u + 1)], ident[:])
-            ht[t, bs] = acc
+            ht[ts, b] = acc
 
-        def interleave(t, bs):
-            tile = keep.tile([P, len(bs), TOK, 2], F32, name="hq%d_%d" % (t, bs[0]), align_bytes=64)
-            nc.scalar.copy(tile[:], ht[t, bs][:].rearrange("p b u j -> p b j u"))
-            hq[t, bs] = tile
+        def interleave(ts, b):
+            tile = keep.tile([P, len(ts), TOK, 2], F32, name="hq%d_%d" % (ts[0], b), align_bytes=64)
+            nc.scalar.copy(tile[:], ht[ts, b][:].rearrange("p t u j -> p t j u"))
+            hq[ts, b] = tile
 
-        def quantise(t, bs):
-            c = keep.tile([P, len(bs) * TOK], U32, name="codes%d_%d" % (t, bs[0]), align_bytes=64)
-            s = keep.tile([P, len(bs) * TOK], U8, name="cscales%d_%d" % (t, bs[0]), align_bytes=64)
+        def quantise(ts, b):
+            c = keep.tile([P, len(ts) * TOK], U32, name="codes%d_%d" % (ts[0], b), align_bytes=64)
+            s = keep.tile([P, len(ts) * TOK], U8, name="cscales%d_%d" % (ts[0], b), align_bytes=64)
             nc.vector.quantize_mx(
                 out=c[:].bitcast(FP8X4),
                 scales=s[:],
-                in_=hq[t, bs][:].rearrange("p b j u -> p (b j u)").bitcast(BF16),
+                in_=hq[ts, b][:].rearrange("p t j u -> p (t j u)").bitcast(BF16),
             )
-            for i, b in enumerate(bs):
+            for i, t in enumerate(ts):
                 codes[t, b] = c[:, TOK * i : TOK * (i + 1)]
                 cscales[t, b] = s[:, TOK * i : TOK * (i + 1)]
 
@@ -156,76 +197,85 @@ def tile_list_gmlpt_relu_mix_none_kernel(
 
         out_v = out.rearrange("(h p) j -> p h j", p=P)
 
-        def second_layer(t):
-            y[t] = psum.tile([P, 2, TOK], F32, name="y", tag="y")
-            for half in range(2):
-                for b in range(HALVES):
-                    down_pass(y[t][:, half, :], t, b, half)
+        def second_layer(ts):
+            y = psum.tile([P, 2, len(ts), TOK], F32, name="y", tag="bank")
+            for i, t in enumerate(ts):
+                for half in range(2):
+                    for b in range(HALVES):
+                        down_pass(y[:, half, i, :], t, b, half)
+            return y
 
-        def store(t, engine_copy):
-            res = keep.tile([P, 2, TOK], F32, name="res%d" % t)
-            engine_copy(res[:], y[t][:])
-            nc.sync.dma_start(out_v[:, :, TOK * t : TOK * (t + 1)], res[:])
+        def store(ts, y, engine_copy):
+            res = keep.tile([P, 2, len(ts) * TOK], F32, name="res%d" % ts[0])
+            engine_copy(res[:], y[:].rearrange("p h t j -> p h (t j)"))
+            nc.sync.dma_start(out_v[:, :, TOK * ts[0] : TOK * (ts[-1] + 1)], res[:])
 
-        both = (0, 1)
-        last = TILES - 1
-        gather(0)
-        first_layer(0, 0)
-        gather(1)
+        lo, hi = (0, 1), (2, 3)
+        GROUP = {0: lo, 1: lo, 2: (2,), 3: (3,)}
+        wg_hi_w = part_words("wg_hi_w", wg_w[:, 2 * PASS : 4 * PASS])
+        for t in range(TILES):
+            gather_scales(t)
+        for t in range(TILES):
+            gather_words(t)
+        wg_hi_s = part_scales("wg_hi_s", wg_s)
+        wu_hi_s = part_scales("wu_hi_s", wu_s)
+        wu_hi_w = part_words("wu_hi_w", wu_hi[:])
+        gate_product(0, 0)
+        up_product(0, 0)
+        gate_product(1, 0)
+        up_product(1, 0)
         rectify(0, 0)
-        first_layer(0, 1)
-        gather(2)
+        gate_product(2, 0)
+        up_product(2, 0)
         multiply(0, 0)
-        rectify(0, 1)
-        first_layer(1, 0)
-        gather(3)
-        multiply(0, 1)
         rectify(1, 0)
-        first_layer(1, 1)
-        turn(0, both)
+        gate_product(3, 0)
+        up_product(3, 0)
         multiply(1, 0)
-        rectify(1, 1)
-        first_layer(2, 0)
-        interleave(0, both)
-        multiply(1, 1)
         rectify(2, 0)
-        first_layer(2, 1)
-        turn(1, both)
-        quantise(0, both)
+        turn(lo, 0)
+        gate_product(0, 1)
+        up_product(0, 1)
         multiply(2, 0)
-        rectify(2, 1)
-        first_layer(3, 0)
-        second_layer(0)
-        interleave(1, both)
-        multiply(2, 1)
         rectify(3, 0)
-        first_layer(3, 1)
-        turn(2, both)
-        store(0, nc.vector.tensor_copy)
-        quantise(1, both)
+        gate_product(1, 1)
+        up_product(1, 1)
         multiply(3, 0)
+        rectify(0, 1)
+        interleave(lo, 0)
+        turn(hi, 0)
+        gate_product(2, 1)
+        up_product(2, 1)
+        multiply(0, 1)
+        rectify(1, 1)
+        quantise(lo, 0)
+        interleave(hi, 0)
+        gate_product(3, 1)
+        up_product(3, 1)
+        multiply(1, 1)
+        rectify(2, 1)
+        quantise(hi, 0)
+        multiply(2, 1)
         rectify(3, 1)
-        second_layer(1)
-        turn(last, (0,))
-        interleave(2, both)
+        quantise(lo, 1)
         multiply(3, 1)
-        turn(last, (1,))
-        interleave(last, (0,))
-        quantise(2, both)
-        store(1, nc.vector.tensor_copy)
-        second_layer(2)
-        interleave(last, (1,))
-        quantise(last, (0,))
-        store(2, nc.scalar.copy)
-        quantise(last, (1,))
-        ya = psum.tile([P, TOK], F32, name="ya", tag="gate")
-        yb = psum.tile([P, TOK], F32, name="yb", tag="up")
-        for b in range(HALVES):
-            down_pass(ya[:], last, b, 0)
-            down_pass(yb[:], last, b, 1)
+        y_0 = second_layer((0,))
+        y_1 = second_layer((1,))
+        quantise((2,), 1)
+        y_2 = second_layer((2,))
+        store((0,), y_0, nc.scalar.copy)
+        store((1,), y_1, nc.scalar.copy)
+        quantise((3,), 1)
+        ya = psum.tile([P, TOK], F32, name="ya", tag="bank")
+        yb = psum.tile([P, TOK], F32, name="yb", tag="bank")
+        down_pass(ya[:], 3, 0, 0)
+        down_pass(yb[:], 3, 0, 1)
+        store((2,), y_2, nc.scalar.copy)
+        down_pass(ya[:], 3, 1, 0)
+        down_pass(yb[:], 3, 1, 1)
         res_a = keep.tile([P, TOK], F32, name="res_a")
         res_b = keep.tile([P, TOK], F32, name="res_b")
         nc.vector.tensor_copy(res_a[:], ya[:])
-        nc.sync.dma_start(out_v[:, 0, TOK * last : TOK * (last + 1)], res_a[:])
+        nc.sync.dma_start(out_v[:, 0, TOK * 3 : TOK * 4], res_a[:])
         nc.scalar.copy(res_b[:], yb[:])
-        nc.scalar.dma_start(out_v[:, 1, TOK * last : TOK * (last + 1)], res_b[:])
+        nc.scalar.dma_start(out_v[:, 1, TOK * 3 : TOK * 4], res_b[:])

@@ -54,6 +54,11 @@ def tile_list_gmlpt_relu_mix_none_kernel(
         ident = keep.tile([P, P], F32, name="ident", align_bytes=64)
         nc.vector.memset(ident[:], 0.0)
         wg_s = plane("wg_s", R)
+        zeros = keep.tile([P, 2 * P], I32, name="zeros", align_bytes=64)
+        nc.vector.memset(zeros[:], 0)
+        zero_w = keep.tile([P, P], U32, name="zero_w", align_bytes=64)
+        zero_s = keep.tile([P, P], U8, name="zero_s", align_bytes=64)
+        nc.vector.quantize_mx(out=zero_w[:].bitcast(FP8X4), scales=zero_s[:], in_=zeros[:].bitcast(BF16))
         wd8_s = plane("wd8_s", N)
         wd4_s = plane("wd4_s", N)
         for q in range(4):
@@ -70,7 +75,14 @@ def tile_list_gmlpt_relu_mix_none_kernel(
         nc.sync.dma_start(wu_hi[:].bitcast(I32), wu_words[0, :, 2 * PASS : 4 * PASS].bitcast(I32))
 
         warm_pe = psum.tile([P, 4, P], F32, name="warm_pe", tag="bank")
-        for i in range(24):
+        for i in range(6):
+            nc.tensor.transpose(warm_pe[:, i % 4, :], ident[:], ident[:])
+        for i in range(8):
+            nc.tensor.matmul_mx(
+                out=warm_pe[:, i % 4, :], lhsT=zero_w[:].bitcast(FP8X4), lhsT_scale=zero_s[:],
+                rhs=zero_w[:].bitcast(FP8X4), rhs_scale=zero_s[:], start=True, stop=True,
+            )
+        for i in range(6):
             nc.tensor.transpose(warm_pe[:, i % 4, :], ident[:], ident[:])
         make_identity(nc, ident[:], nomemset=True)
         wd8_w = keep.tile([P, N], I32, name="wd8_w", align_bytes=64)

@@ -39,21 +39,19 @@ def tile_list_gmlpt_relu_mix_none_kernel(
             nc.vector.memset(tile[:], 0)
             return tile
 
-        def load_rows(tile, scales, q):
-            nc.sync.dma_start(tile[32 * q : 32 * q + 4, :], scales[0, 4 * q : 4 * q + 4, :].bitcast(I32))
+        def load_rows(tile, scales, q, queue=nc.sync):
+            queue.dma_start(tile[32 * q : 32 * q + 4, :], scales[0, 4 * q : 4 * q + 4, :].bitcast(I32))
 
         offsets = keep.tile([P, J // 16], U16, name="offsets")
         nc.sync.dma_start(offsets[:], offs)
         wg_w = keep.tile([P, 2 * R], U8, name="wg_w", align_bytes=64)
-        nc.sync.dma_start(wg_w[:].bitcast(I32), wg_words[0].bitcast(I32))
-        wu_lo = keep.tile([P, 2 * PASS], U8, name="wu_lo", align_bytes=64)
-        nc.gpsimd.dma_start(wu_lo[:].bitcast(I32), wu_words[0, :, 0 : 2 * PASS].bitcast(I32))
+        nc.scalar.dma_start(wg_w[:].bitcast(I32), wg_words[0].bitcast(I32))
+        wu_w = keep.tile([P, 2 * R], U8, name="wu_w", align_bytes=64)
+        nc.gpsimd.dma_start(wu_w[:].bitcast(I32), wu_words[0].bitcast(I32))
 
         tab_s = plane("tab_s", T)
-        wu_s = plane("wu_s", R)
-        ident = keep.tile([P, P], F32, name="ident", align_bytes=64)
-        nc.vector.memset(ident[:], 0.0)
         wg_s = plane("wg_s", R)
+        wu_s = plane("wu_s", R)
         zeros = keep.tile([P, 2 * P], I32, name="zeros", align_bytes=64)
         nc.vector.memset(zeros[:], 0)
         zero_w = keep.tile([P, P], U32, name="zero_w", align_bytes=64)
@@ -62,33 +60,29 @@ def tile_list_gmlpt_relu_mix_none_kernel(
         wd8_s = plane("wd8_s", N)
         wd4_s = plane("wd4_s", N)
         for q in range(4):
-            load_rows(tab_s, tab_scales, q)
-        load_rows(wu_s, wu_scales, 0)
-        tab_w = keep.tile([P, T], I32, name="tab_w", align_bytes=64)
+            load_rows(tab_s, tab_scales, q, nc.sync if q == 1 else nc.scalar)
+        load_rows(wg_s, wg_scales, 0)
+        tab_w = keep.tile([P, T], I32, name="tab_w", tag="tab_w", align_bytes=64)
         nc.sync.dma_start(tab_w[:], tab_words[0].rearrange("p t i -> p (t i)").bitcast(I32))
-        load_rows(wu_s, wu_scales, 1)
-        load_rows(wu_s, wu_scales, 2)
-        for q in range(4):
-            load_rows(wg_s, wg_scales, q)
-        load_rows(wu_s, wu_scales, 3)
-        wu_hi = keep.tile([P, 2 * PASS], U8, name="wu_hi", align_bytes=64)
-        nc.sync.dma_start(wu_hi[:].bitcast(I32), wu_words[0, :, 2 * PASS : 4 * PASS].bitcast(I32))
+        load_rows(wu_s, wu_scales, 0, nc.scalar)
+        load_rows(wg_s, wg_scales, 1, nc.scalar)
+        load_rows(wg_s, wg_scales, 2)
+        load_rows(wg_s, wg_scales, 3)
+        for q in range(1, 4):
+            load_rows(wu_s, wu_scales, q, nc.scalar)
 
-        warm_pe = psum.tile([P, 4, P], F32, name="warm_pe", tag="bank")
-        for i in range(6):
-            nc.tensor.transpose(warm_pe[:, i % 4, :], ident[:], ident[:])
-        for i in range(8):
+        warm_pe = psum.tile([P, PASS], F32, name="warm_pe", tag="bank")
+        for i in range(2):
             nc.tensor.matmul_mx(
-                out=warm_pe[:, i % 4, :], lhsT=zero_w[:].bitcast(FP8X4), lhsT_scale=zero_s[:],
-                rhs=zero_w[:].bitcast(FP8X4), rhs_scale=zero_s[:], start=True, stop=True,
+                out=warm_pe[:], lhsT=zero_w[:].bitcast(FP8X4), lhsT_scale=zero_s[:],
+                rhs=wg_w[:, 0 : 2 * PASS].bitcast(FP4X4), rhs_scale=tab_s[:].bitcast(U8)[:, 0:PASS], start=True, stop=True,
             )
-        for i in range(6):
-            nc.tensor.transpose(warm_pe[:, i % 4, :], ident[:], ident[:])
-        make_identity(nc, ident[:], nomemset=True)
+        ident = keep.tile([P, P], F32, name="ident", align_bytes=64)
+        make_identity(nc, ident[:])
         wd8_w = keep.tile([P, N], I32, name="wd8_w", align_bytes=64)
-        nc.gpsimd.dma_start(wd8_w[:], wd8_words[0].rearrange("p n i -> p (n i)").bitcast(I32))
+        nc.sync.dma_start(wd8_w[:], wd8_words[0].rearrange("p n i -> p (n i)").bitcast(I32))
         wd4_w = keep.tile([P, 2 * N], U8, name="wd4_w", align_bytes=64)
-        nc.gpsimd.dma_start(wd4_w[:].bitcast(I32), wd4_words[0].bitcast(I32))
+        nc.sync.dma_start(wd4_w[:].bitcast(I32), wd4_words[0].bitcast(I32))
         for q in range(4):
             load_rows(wd8_s, wd8_scales, q)
         for q in range(4):
@@ -96,16 +90,18 @@ def tile_list_gmlpt_relu_mix_none_kernel(
 
         v_w, v_s, gate, up, relu, h, ht, hq, codes, cscales = ({} for i in range(10))
 
-        def gather_scales(t):
-            v_s[t] = keep.tile([P, TOK], U8, name="v_s%d" % t, align_bytes=64)
-            nc.vector.tensor_copy(v_s[t][:], tab_s[:].bitcast(U8).indirect(offsets[:, t * TOK // 16 : (t + 1) * TOK // 16]))
+        def gather_scales():
+            picked = keep.tile([P, J], U8, name="v_s", align_bytes=64)
+            nc.vector.tensor_copy(picked[:], tab_s[:].bitcast(U8).indirect(offsets[:]))
+            for t in range(TILES):
+                v_s[t] = picked[:, TOK * t : TOK * (t + 1)]
 
         def gather_words(t):
             v_w[t] = keep.tile([P, TOK], U32, name="v_w%d" % t, align_bytes=64)
             nc.vector.tensor_copy(v_w[t][:], tab_w[:].bitcast(U32).indirect(offsets[:, t * TOK // 16 : (t + 1) * TOK // 16]))
 
-        def part_words(name, words):
-            tile = keep.tile([P, 2 * PASS], U8, name=name, align_bytes=64)
+        def part_words(name, words, tag):
+            tile = keep.tile([P, 2 * PASS], U8, name=name, tag=tag, align_bytes=64)
             nc.vector.tensor_copy(
                 tile[:].bitcast(U16).rearrange("p (i c m) -> p c i m", i=4, m=8),
                 words.bitcast(U16).rearrange("p (c m i) -> p c i m", i=4, m=8),
@@ -125,7 +121,7 @@ def tile_list_gmlpt_relu_mix_none_kernel(
             nc.tensor.matmul_mx(
                 out=acc[:],
                 lhsT=v_w[t][:].bitcast(FP8X4),
-                lhsT_scale=v_s[t][:],
+                lhsT_scale=v_s[t],
                 rhs=words.bitcast(FP4X4),
                 rhs_scale=scales[:].bitcast(U8)[:, 0:PASS],
                 start=True,
@@ -141,7 +137,7 @@ def tile_list_gmlpt_relu_mix_none_kernel(
                     lhsT=words[:, 2 * P * i : 2 * P * (i + 1)].bitcast(FP4X4),
                     lhsT_scale=scales[:, P * i : P * (i + 1)],
                     rhs=v_w[t][:].bitcast(FP8X4),
-                    rhs_scale=v_s[t][:],
+                    rhs_scale=v_s[t],
                     start=True,
                     stop=True,
                 )
@@ -151,10 +147,10 @@ def tile_list_gmlpt_relu_mix_none_kernel(
             gate[t, b] = product_hi(t, wg_hi_w, wg_hi_s) if b else product_lo(t, wg_w[:, 0 : 2 * PASS], wg_s)
 
         def up_product(t, b):
-            up[t, b] = product_hi(t, wu_hi_w, wu_hi_s) if b else product_lo(t, wu_lo[:], wu_s)
+            up[t, b] = product_hi(t, wu_hi_w, wu_hi_s) if b else product_lo(t, wu_w[:, 0 : 2 * PASS], wu_s)
 
         def rectify(t, b):
-            relu[t, b] = keep.tile([P, TOK, 4] if b else [P, 2, P, 2], F32, name="relu%d_%d" % (t, b))
+            relu[t, b] = keep.tile([P, TOK, 4] if b else [P, 2, P, 2], F32, name="relu%d_%d" % (t, b), tag="relu%d_%d" % (t, b), align_bytes=64)
             nc.scalar.activation(relu[t, b][:], gate[t, b], RELU)
 
         def multiply(t, b):
@@ -224,52 +220,40 @@ def tile_list_gmlpt_relu_mix_none_kernel(
 
         lo, hi = (0, 1), (2, 3)
         GROUP = {0: lo, 1: lo, 2: (2,), 3: (3,)}
-        wg_hi_w = part_words("wg_hi_w", wg_w[:, 2 * PASS : 4 * PASS])
-        for t in range(TILES):
-            gather_scales(t)
+        wg_hi_w = part_words("wg_hi_w", wg_w[:, 2 * PASS : 4 * PASS], "wg_hi_w")
+        gather_scales()
         for t in range(TILES):
             gather_words(t)
+        wu_hi_w = part_words("wu_hi_w", wu_w[:, 2 * PASS : 4 * PASS], "tab_w")
         wg_hi_s = part_scales("wg_hi_s", wg_s)
         wu_hi_s = part_scales("wu_hi_s", wu_s)
-        wu_hi_w = part_words("wu_hi_w", wu_hi[:])
-        gate_product(0, 0)
-        up_product(0, 0)
-        gate_product(1, 0)
-        up_product(1, 0)
-        rectify(0, 0)
-        gate_product(2, 0)
-        up_product(2, 0)
-        multiply(0, 0)
-        rectify(1, 0)
-        gate_product(3, 0)
-        up_product(3, 0)
-        multiply(1, 0)
-        rectify(2, 0)
-        turn(lo, 0)
+        for t in range(TILES):
+            gate_product(t, 0)
+            up_product(t, 0)
+            rectify(t, 0)
+            multiply(t, 0)
         gate_product(0, 1)
         up_product(0, 1)
-        multiply(2, 0)
-        rectify(3, 0)
+        rectify(0, 1)
+        multiply(0, 1)
+        turn(lo, 0)
+        interleave(lo, 0)
+        quantise(lo, 0)
         gate_product(1, 1)
         up_product(1, 1)
-        multiply(3, 0)
-        rectify(0, 1)
-        interleave(lo, 0)
-        turn(hi, 0)
-        gate_product(2, 1)
-        up_product(2, 1)
-        multiply(0, 1)
         rectify(1, 1)
-        quantise(lo, 0)
-        interleave(hi, 0)
-        gate_product(3, 1)
-        up_product(3, 1)
         multiply(1, 1)
-        rectify(2, 1)
+        turn(hi, 0)
+        interleave(hi, 0)
         quantise(hi, 0)
-        multiply(2, 1)
+        gate_product(2, 1)
+        gate_product(3, 1)
+        up_product(2, 1)
+        up_product(3, 1)
+        rectify(2, 1)
         rectify(3, 1)
         quantise(lo, 1)
+        multiply(2, 1)
         multiply(3, 1)
         y_0 = second_layer((0,))
         y_1 = second_layer((1,))

@@ -67,9 +67,10 @@ def tile_list_gmlpt_relu_mix_none_kernel(
         load_rows(wu_s, wu_scales, 0, nc.scalar)
         load_rows(wg_s, wg_scales, 1, nc.scalar)
         load_rows(wg_s, wg_scales, 2)
-        load_rows(wg_s, wg_scales, 3)
-        for q in range(1, 4):
-            load_rows(wu_s, wu_scales, q, nc.scalar)
+        load_rows(wu_s, wu_scales, 1, nc.scalar)
+        load_rows(wu_s, wu_scales, 2)
+        load_rows(wg_s, wg_scales, 3, nc.scalar)
+        load_rows(wu_s, wu_scales, 3, nc.scalar)
 
         warm_pe = psum.tile([P, PASS], F32, name="warm_pe", tag="bank")
         for i in range(2):
@@ -100,21 +101,20 @@ def tile_list_gmlpt_relu_mix_none_kernel(
             v_w[t] = keep.tile([P, TOK], U32, name="v_w%d" % t, align_bytes=64)
             nc.vector.tensor_copy(v_w[t][:], tab_w[:].bitcast(U32).indirect(offsets[:, t * TOK // 16 : (t + 1) * TOK // 16]))
 
-        def part_words(name, words, tag):
-            tile = keep.tile([P, 2 * PASS], U8, name=name, tag=tag, align_bytes=64)
-            nc.vector.tensor_copy(
-                tile[:].bitcast(U16).rearrange("p (i c m) -> p c i m", i=4, m=8),
-                words.bitcast(U16).rearrange("p (c m i) -> p c i m", i=4, m=8),
+        def part(engine, name, source, dtype, tag):
+            tile = keep.tile([P, PASS], dtype, name=name, tag=tag, align_bytes=64)
+            run = 128 if engine is nc.gpsimd else 8 if dtype == U16 else 16
+            engine.tensor_copy(
+                tile[:].rearrange("p (i c m) -> p c i m", i=4, m=run),
+                source.rearrange("p (c m i) -> p c i m", i=4, m=run),
             )
-            return tile
+            return tile[:].bitcast(U8)
 
-        def part_scales(name, scales):
-            tile = keep.tile([P, PASS], U8, name=name, align_bytes=64)
-            nc.vector.tensor_copy(
-                tile[:].rearrange("p (i c m) -> p c i m", i=4, m=16),
-                scales[:].bitcast(U8)[:, PASS : 2 * PASS].rearrange("p (c m i) -> p c i m", i=4, m=16),
-            )
-            return tile
+        def part_words(engine, name, words, b, tag):
+            return part(engine, name, words[:].bitcast(U16)[:, PASS * b : PASS * (b + 1)], U16, tag)
+
+        def part_scales(engine, name, scales, b, tag):
+            return part(engine, name, scales[:].bitcast(U8)[:, PASS * b : PASS * (b + 1)], U8, tag)
 
         def product_lo(t, words, scales):
             acc = psum.tile([P, PASS], F32, name="acc", tag="bank")
@@ -143,25 +143,27 @@ def tile_list_gmlpt_relu_mix_none_kernel(
                 )
             return acc[:].rearrange("p i j -> p j i")
 
+        def turned(t, b):
+            return b == 0 and t in lo
+
         def gate_product(t, b):
-            gate[t, b] = product_hi(t, wg_hi_w, wg_hi_s) if b else product_lo(t, wg_w[:, 0 : 2 * PASS], wg_s)
+            gate[t, b] = product_lo(t, wg_w[:, 0 : 2 * PASS], wg_s) if turned(t, b) else product_hi(t, gw[b], gs[b])
 
         def up_product(t, b):
-            up[t, b] = product_hi(t, wu_hi_w, wu_hi_s) if b else product_lo(t, wu_w[:, 0 : 2 * PASS], wu_s)
+            up[t, b] = product_lo(t, wu_w[:, 0 : 2 * PASS], wu_s) if turned(t, b) else product_hi(t, uw[b], us[b])
 
         def rectify(t, b):
-            relu[t, b] = keep.tile([P, TOK, 4] if b else [P, 2, P, 2], F32, name="relu%d_%d" % (t, b), tag="relu%d_%d" % (t, b), align_bytes=64)
+            relu[t, b] = keep.tile([P, 2, P, 2] if turned(t, b) else [P, TOK, 4], F32, name="relu%d_%d" % (t, b), tag="relu%d_%d" % (t, b), align_bytes=64)
             nc.scalar.activation(relu[t, b][:], gate[t, b], RELU)
 
-        def multiply(t, b):
-            if b:
-                ts = GROUP[t]
-                if (ts, b) not in hq:
-                    hq[ts, b] = keep.tile([P, len(ts), TOK, 2], F32, name="hq%d_1" % t, align_bytes=64)
-                dst = hq[ts, b][:, ts.index(t)].bitcast(BF16)
-            else:
+        def multiply(t, b, ts):
+            if turned(t, b):
                 h[t, b] = keep.tile([P, 2, P, 2], BF16, name="h%d_%d" % (t, b), align_bytes=64)
                 dst = h[t, b][:]
+            else:
+                if (ts, b) not in hq:
+                    hq[ts, b] = keep.tile([P, len(ts), TOK, 2], F32, name="hq%d_%d" % (t, b), align_bytes=64)
+                dst = hq[ts, b][:, ts.index(t)].bitcast(BF16)
             nc.vector.tensor_tensor(dst, up[t, b], relu[t, b][:], MULT)
 
         def turn(ts, b):
@@ -189,7 +191,7 @@ def tile_list_gmlpt_relu_mix_none_kernel(
                 codes[t, b] = c[:, TOK * i : TOK * (i + 1)]
                 cscales[t, b] = s[:, TOK * i : TOK * (i + 1)]
 
-        def down_pass(acc, t, b, half):
+        def down_pass(acc, t, b, half, first):
             n0 = P * half
             if b == 0:
                 lhs = wd8_w[:, n0 : n0 + P].bitcast(FP8X4)
@@ -200,7 +202,7 @@ def tile_list_gmlpt_relu_mix_none_kernel(
             nc.tensor.matmul_mx(
                 out=acc, lhsT=lhs, lhsT_scale=lhs_s,
                 rhs=codes[t, b].bitcast(FP8X4), rhs_scale=cscales[t, b],
-                start=(b == 0), stop=(b == 1),
+                start=(b == first), stop=(b != first),
             )
 
         out_v = out.rearrange("(h p) j -> p h j", p=P)
@@ -210,7 +212,7 @@ def tile_list_gmlpt_relu_mix_none_kernel(
             for i, t in enumerate(ts):
                 for half in range(2):
                     for b in range(HALVES):
-                        down_pass(y[:, half, i, :], t, b, half)
+                        down_pass(y[:, half, i, :], t, b, half, 0)
             return y
 
         def store(ts, y, engine_copy):
@@ -219,56 +221,60 @@ def tile_list_gmlpt_relu_mix_none_kernel(
             nc.sync.dma_start(out_v[:, :, TOK * ts[0] : TOK * (ts[-1] + 1)], res[:])
 
         lo, hi = (0, 1), (2, 3)
-        GROUP = {0: lo, 1: lo, 2: (2,), 3: (3,)}
-        wg_hi_w = part_words("wg_hi_w", wg_w[:, 2 * PASS : 4 * PASS], "wg_hi_w")
+        gw, uw, gs, us = {}, {}, {}, {}
+        gw[1] = part_words(nc.vector, "wg_hi_w", wg_w, 1, "wg_hi_w")
+        gw[0] = part_words(nc.gpsimd, "wg_lo_w", wg_w, 0, "wg_lo_w")
         gather_scales()
         for t in range(TILES):
             gather_words(t)
-        wu_hi_w = part_words("wu_hi_w", wu_w[:, 2 * PASS : 4 * PASS], "tab_w")
-        wg_hi_s = part_scales("wg_hi_s", wg_s)
-        wu_hi_s = part_scales("wu_hi_s", wu_s)
-        for t in range(TILES):
-            gate_product(t, 0)
-            up_product(t, 0)
-            rectify(t, 0)
-            multiply(t, 0)
-        gate_product(0, 1)
-        up_product(0, 1)
-        rectify(0, 1)
-        multiply(0, 1)
+        uw[1] = part_words(nc.vector, "wu_hi_w", wu_w, 1, "tab_w")
+        gs[1] = part_scales(nc.gpsimd, "wg_hi_s", wg_s, 1, "wg_hi_s")
+        us[1] = part_scales(nc.gpsimd, "wu_hi_s", wu_s, 1, "wu_hi_s")
+        gate_product(0, 0)
+        up_product(0, 0)
+        relu[0, 0] = keep.tile([P, 2, P, 2], F32, name="relu0_0", tag="relu0_0", align_bytes=64)
+        h[0, 0] = keep.tile([P, 2, P, 2], BF16, name="h0_0", align_bytes=64)
+        for u in range(2):
+            nc.scalar.activation(relu[0, 0][:, u], gate[0, 0][:, u], RELU)
+            nc.vector.tensor_tensor(h[0, 0][:, u], up[0, 0][:, u], relu[0, 0][:, u], MULT)
+        gate_product(1, 0)
+        up_product(1, 0)
+        rectify(1, 0)
+        multiply(1, 0, lo)
+        uw[0] = part_words(nc.gpsimd, "wu_lo_w", wu_w, 0, "relu0_0")
+        gs[0] = part_scales(nc.gpsimd, "wg_lo_s", wg_s, 0, "relu1_0")
+        us[0] = part_scales(nc.gpsimd, "wu_lo_s", wu_s, 0, "wu_lo_s")
+        for t in lo:
+            gate_product(t, 1)
+            up_product(t, 1)
+            rectify(t, 1)
+            multiply(t, 1, lo)
         turn(lo, 0)
         interleave(lo, 0)
-        quantise(lo, 0)
-        gate_product(1, 1)
-        up_product(1, 1)
-        rectify(1, 1)
-        multiply(1, 1)
-        turn(hi, 0)
-        interleave(hi, 0)
-        quantise(hi, 0)
-        gate_product(2, 1)
-        gate_product(3, 1)
-        up_product(2, 1)
-        up_product(3, 1)
-        rectify(2, 1)
-        rectify(3, 1)
+        for t in hi:
+            gate_product(t, 1)
+            up_product(t, 1)
+            rectify(t, 1)
+            multiply(t, 1, hi)
         quantise(lo, 1)
-        multiply(2, 1)
-        multiply(3, 1)
-        y_0 = second_layer((0,))
-        y_1 = second_layer((1,))
-        quantise((2,), 1)
-        y_2 = second_layer((2,))
-        store((0,), y_0, nc.scalar.copy)
-        store((1,), y_1, nc.scalar.copy)
-        quantise((3,), 1)
+        quantise(lo, 0)
+        for t in hi:
+            gate_product(t, 0)
+        for t in hi:
+            up_product(t, 0)
+            rectify(t, 0)
+        multiply(2, 0, (2,))
+        quantise(hi, 1)
+        quantise((2,), 0)
+        multiply(3, 0, (3,))
+        quantise((3,), 0)
+        for t in range(TILES - 1):
+            store((t,), second_layer((t,)), nc.scalar.copy)
         ya = psum.tile([P, TOK], F32, name="ya", tag="bank")
         yb = psum.tile([P, TOK], F32, name="yb", tag="bank")
-        down_pass(ya[:], 3, 0, 0)
-        down_pass(yb[:], 3, 0, 1)
-        store((2,), y_2, nc.scalar.copy)
-        down_pass(ya[:], 3, 1, 0)
-        down_pass(yb[:], 3, 1, 1)
+        for b in (1, 0):
+            for half, y in enumerate((ya, yb)):
+                down_pass(y[:], 3, b, half, 1)
         res_a = keep.tile([P, TOK], F32, name="res_a")
         res_b = keep.tile([P, TOK], F32, name="res_b")
         nc.vector.tensor_copy(res_a[:], ya[:])

@@ -40,7 +40,7 @@ def tile_list_gmlpt_relu_mix_none_kernel(
             return tile
 
         def load_rows(tile, scales, q, queue=nc.sync):
-            queue.dma_start(tile[32 * q : 32 * q + 4, :], scales[0, 4 * q : 4 * q + 4, :].bitcast(I32))
+            queue.dma_start(tile[q : P : 32, :], scales[0, q : 16 : 4, :].bitcast(I32))
 
         offsets = keep.tile([P, J // 16], U16, name="offsets")
         nc.sync.dma_start(offsets[:], offs)
@@ -64,13 +64,11 @@ def tile_list_gmlpt_relu_mix_none_kernel(
         load_rows(wg_s, wg_scales, 0)
         tab_w = keep.tile([P, T], I32, name="tab_w", tag="tab_w", align_bytes=64)
         nc.sync.dma_start(tab_w[:], tab_words[0].rearrange("p t i -> p (t i)").bitcast(I32))
-        load_rows(wu_s, wu_scales, 0, nc.scalar)
         load_rows(wg_s, wg_scales, 1, nc.scalar)
         load_rows(wg_s, wg_scales, 2)
-        load_rows(wu_s, wu_scales, 1, nc.scalar)
-        load_rows(wu_s, wu_scales, 2)
-        load_rows(wg_s, wg_scales, 3, nc.scalar)
-        load_rows(wu_s, wu_scales, 3, nc.scalar)
+        load_rows(wg_s, wg_scales, 3)
+        for q in range(4):
+            load_rows(wu_s, wu_scales, q, nc.scalar)
 
         warm_pe = psum.tile([P, PASS], F32, name="warm_pe", tag="bank")
         for i in range(2):

@@ -247,14 +247,15 @@ def tile_list_gmlpt_relu_mix_none_kernel(
             up_product(t, 1)
             rectify(t, 1)
             multiply(t, 1, lo)
-        turn(lo, 0)
-        interleave(lo, 0)
         for t in hi:
             gate_product(t, 1)
             up_product(t, 1)
             rectify(t, 1)
             multiply(t, 1, hi)
-        quantise(lo, 1)
+            if t == 2:
+                quantise(lo, 1)
+        turn(lo, 0)
+        interleave(lo, 0)
         quantise(lo, 0)
         for t in hi:
             gate_product(t, 0)
@@ -266,16 +267,17 @@ def tile_list_gmlpt_relu_mix_none_kernel(
         quantise((2,), 0)
         multiply(3, 0, (3,))
         quantise((3,), 0)
-        for t in range(TILES - 1):
+        for t in lo:
             store((t,), second_layer((t,)), nc.scalar.copy)
-        ya = psum.tile([P, TOK], F32, name="ya", tag="bank")
-        yb = psum.tile([P, TOK], F32, name="yb", tag="bank")
-        for b in (1, 0):
-            for half, y in enumerate((ya, yb)):
-                down_pass(y[:], 3, b, half, 1)
-        res_a = keep.tile([P, TOK], F32, name="res_a")
-        res_b = keep.tile([P, TOK], F32, name="res_b")
-        nc.vector.tensor_copy(res_a[:], ya[:])
-        nc.sync.dma_start(out_v[:, 0, TOK * 3 : TOK * 4], res_a[:])
-        nc.scalar.copy(res_b[:], yb[:])
-        nc.scalar.dma_start(out_v[:, 1, TOK * 3 : TOK * 4], res_b[:])
+        y = {}
+        for t in hi:
+            for half in range(2):
+                y[t, half] = psum.tile([P, TOK], F32, name="y%d_%d" % (t, half), tag="bank")
+                down_pass(y[t, half][:], t, 1, half, 1)
+        for t in hi:
+            for half in range(2):
+                down_pass(y[t, half][:], t, 0, half, 1)
+            for half, copy, queue in ((0, nc.vector.tensor_copy, nc.sync), (1, nc.scalar.copy, nc.scalar)):
+                res = keep.tile([P, TOK], F32, name="res%d_%d" % (t, half))
+                copy(res[:], y[t, half][:])
+                queue.dma_start(out_v[:, half, TOK * t : TOK * (t + 1)], res[:])

@@ -31,7 +31,7 @@ def tile_list_gmlpt_relu_mix_none_kernel(
     nc = tc.nc
     with ExitStack() as ctx:
         keep = ctx.enter_context(tc.tile_pool(name="keep", bufs=1))
-        ring = ctx.enter_context(tc.tile_pool(name="ring", bufs=2))
+        reuse = ctx.enter_context(tc.tile_pool(name="reuse", bufs=1))
         psum = ctx.enter_context(tc.psum_pool(name="psum", bufs=8))
 
         def plane(name, width):
@@ -62,7 +62,7 @@ def tile_list_gmlpt_relu_mix_none_kernel(
         for q in range(4):
             load_rows(tab_s, tab_scales, q, nc.sync if q == 1 else nc.scalar)
         load_rows(wg_s, wg_scales, 0)
-        tab_w = keep.tile([P, T], I32, name="tab_w", tag="tab_w", align_bytes=64)
+        tab_w = reuse.tile([P, T], I32, name="tab_w", align_bytes=64, offset=0)
         nc.sync.dma_start(tab_w[:], tab_words[0].rearrange("p t i -> p (t i)").bitcast(I32))
         load_rows(wg_s, wg_scales, 1, nc.scalar)
         load_rows(wg_s, wg_scales, 2)
@@ -89,18 +89,21 @@ def tile_list_gmlpt_relu_mix_none_kernel(
 
         v_w, v_s, gate, up, relu, h, ht, hq, codes, cscales = ({} for i in range(10))
 
-        def gather_scales():
-            picked = keep.tile([P, J], U8, name="v_s", align_bytes=64)
-            nc.vector.tensor_copy(picked[:], tab_s[:].bitcast(U8).indirect(offsets[:]))
-            for t in range(TILES):
-                v_s[t] = picked[:, TOK * t : TOK * (t + 1)]
+        def gather_scales(ts, picked):
+            cols = slice(ts[0] * TOK // 16, (ts[-1] + 1) * TOK // 16)
+            nc.vector.tensor_copy(picked[:], tab_s[:].bitcast(U8).indirect(offsets[:, cols]))
+            for i, t in enumerate(ts):
+                v_s[t] = picked[:, TOK * i : TOK * (i + 1)]
 
         def gather_words(t):
             v_w[t] = keep.tile([P, TOK], U32, name="v_w%d" % t, align_bytes=64)
             nc.vector.tensor_copy(v_w[t][:], tab_w[:].bitcast(U32).indirect(offsets[:, t * TOK // 16 : (t + 1) * TOK // 16]))
 
         def part(engine, name, source, dtype, tag):
-            tile = keep.tile([P, PASS], dtype, name=name, tag=tag, align_bytes=64)
+            if tag is None:
+                tile = reuse.tile([P, PASS], dtype, name=name, align_bytes=64, offset=0)
+            else:
+                tile = keep.tile([P, PASS], dtype, name=name, tag=tag, align_bytes=64)
             run = 128 if engine is nc.gpsimd else 8 if dtype == U16 else 16
             engine.tensor_copy(
                 tile[:].rearrange("p (i c m) -> p c i m", i=4, m=run),
@@ -220,12 +223,13 @@ def tile_list_gmlpt_relu_mix_none_kernel(
 
         lo, hi = (0, 1), (2, 3)
         gw, uw, gs, us = {}, {}, {}, {}
-        gw[1] = part_words(nc.vector, "wg_hi_w", wg_w, 1, "wg_hi_w")
+        gw[1] = part_words(nc.gpsimd, "wg_hi_w", wg_w, 1, "wg_hi_w")
         gw[0] = part_words(nc.gpsimd, "wg_lo_w", wg_w, 0, "wg_lo_w")
-        gather_scales()
+        gather_scales((0, 1, 2), keep.tile([P, 3 * TOK], U8, name="v_s", align_bytes=64))
         for t in range(TILES):
             gather_words(t)
-        uw[1] = part_words(nc.vector, "wu_hi_w", wu_w, 1, "tab_w")
+        uw[1] = part_words(nc.vector, "wu_hi_w", wu_w, 1, None)
+        gather_scales((3,), reuse.tile([P, TOK], U8, name="v_s3", align_bytes=64, offset=2 * PASS))
         gs[1] = part_scales(nc.gpsimd, "wg_hi_s", wg_s, 1, "wg_hi_s")
         us[1] = part_scales(nc.gpsimd, "wu_hi_s", wu_s, 1, "wu_hi_s")
         gate_product(0, 0)

@@ -65,10 +65,12 @@ def tile_list_gmlpt_relu_mix_none_kernel(
         tab_w = reuse.tile([P, T], I32, name="tab_w", align_bytes=64, offset=0)
         nc.sync.dma_start(tab_w[:], tab_words[0].rearrange("p t i -> p (t i)").bitcast(I32))
         load_rows(wg_s, wg_scales, 1, nc.scalar)
+        load_rows(wu_s, wu_scales, 0, nc.scalar)
         load_rows(wg_s, wg_scales, 2)
         load_rows(wg_s, wg_scales, 3)
-        for q in range(4):
-            load_rows(wu_s, wu_scales, q, nc.scalar)
+        load_rows(wu_s, wu_scales, 1)
+        load_rows(wu_s, wu_scales, 2)
+        load_rows(wu_s, wu_scales, 3, nc.gpsimd)
 
         warm_pe = psum.tile([P, PASS], F32, name="warm_pe", tag="bank")
         for i in range(2):
@@ -100,12 +102,9 @@ def tile_list_gmlpt_relu_mix_none_kernel(
             nc.vector.tensor_copy(v_w[t][:], tab_w[:].bitcast(U32).indirect(offsets[:, t * TOK // 16 : (t + 1) * TOK // 16]))
 
         def part(engine, name, source, dtype, tag):
-            if tag is None:
-                tile = reuse.tile([P, PASS], dtype, name=name, align_bytes=64, offset=0)
-            else:
-                tile = keep.tile([P, PASS], dtype, name=name, tag=tag, align_bytes=64)
+            tile = keep.tile([P, PASS], dtype, name=name, tag=tag, align_bytes=64)
             run = 128 if engine is nc.gpsimd else 8 if dtype == U16 else 16
-            engine.tensor_copy(
+            (engine.copy if engine is nc.scalar else engine.tensor_copy)(
                 tile[:].rearrange("p (i c m) -> p c i m", i=4, m=run),
                 source.rearrange("p (c m i) -> p c i m", i=4, m=run),
             )
@@ -228,8 +227,8 @@ def tile_list_gmlpt_relu_mix_none_kernel(
         gather_scales((0, 1, 2), keep.tile([P, 3 * TOK], U8, name="v_s", align_bytes=64))
         for t in range(TILES):
             gather_words(t)
-        uw[1] = part_words(nc.vector, "wu_hi_w", wu_w, 1, None)
-        gather_scales((3,), reuse.tile([P, TOK], U8, name="v_s3", align_bytes=64, offset=2 * PASS))
+        uw[1] = part_words(nc.scalar, "wu_hi_w", wu_w, 1, "wu_hi_w")
+        gather_scales((3,), reuse.tile([P, TOK], U8, name="v_s3", align_bytes=64, offset=0))
         gs[1] = part_scales(nc.gpsimd, "wg_hi_s", wg_s, 1, "wg_hi_s")
         us[1] = part_scales(nc.gpsimd, "wu_hi_s", wu_s, 1, "wu_hi_s")
         gate_product(0, 0)

@@ -60,8 +60,8 @@ def tile_list_gmlpt_relu_mix_none_kernel(
         wd8_s = plane("wd8_s", N)
         wd4_s = plane("wd4_s", N)
         for q in range(4):
-            load_rows(tab_s, tab_scales, q, nc.sync if q == 1 else nc.scalar)
-        load_rows(wg_s, wg_scales, 0)
+            load_rows(tab_s, tab_scales, q, nc.sync if q % 2 else nc.scalar)
+        load_rows(wg_s, wg_scales, 0, nc.scalar)
         tab_w = reuse.tile([P, T], I32, name="tab_w", align_bytes=64, offset=0)
         nc.sync.dma_start(tab_w[:], tab_words[0].rearrange("p t i -> p (t i)").bitcast(I32))
         load_rows(wg_s, wg_scales, 1, nc.scalar)
@@ -224,11 +224,11 @@ def tile_list_gmlpt_relu_mix_none_kernel(
         gw, uw, gs, us = {}, {}, {}, {}
         gw[1] = part_words(nc.gpsimd, "wg_hi_w", wg_w, 1, "wg_hi_w")
         gw[0] = part_words(nc.gpsimd, "wg_lo_w", wg_w, 0, "wg_lo_w")
-        gather_scales((0, 1, 2), keep.tile([P, 3 * TOK], U8, name="v_s", align_bytes=64))
+        gather_scales(lo, keep.tile([P, 2 * TOK], U8, name="v_s_lo", align_bytes=64))
         for t in range(TILES):
             gather_words(t)
         uw[1] = part_words(nc.scalar, "wu_hi_w", wu_w, 1, "wu_hi_w")
-        gather_scales((3,), reuse.tile([P, TOK], U8, name="v_s3", align_bytes=64, offset=0))
+        gather_scales(hi, reuse.tile([P, 2 * TOK], U8, name="v_s_hi", align_bytes=64, offset=0))
         gs[1] = part_scales(nc.gpsimd, "wg_hi_s", wg_s, 1, "wg_hi_s")
         us[1] = part_scales(nc.gpsimd, "wu_hi_s", wu_s, 1, "wu_hi_s")
         gate_product(0, 0)

@@ -65,9 +65,9 @@ def tile_list_gmlpt_relu_mix_none_kernel(
         tab_w = reuse.tile([P, T], I32, name="tab_w", align_bytes=64, offset=0)
         nc.sync.dma_start(tab_w[:], tab_words[0].rearrange("p t i -> p (t i)").bitcast(I32))
         load_rows(wg_s, wg_scales, 1, nc.scalar)
-        load_rows(wu_s, wu_scales, 0, nc.scalar)
-        load_rows(wg_s, wg_scales, 2)
+        load_rows(wg_s, wg_scales, 2, nc.scalar)
         load_rows(wg_s, wg_scales, 3)
+        load_rows(wu_s, wu_scales, 0)
         load_rows(wu_s, wu_scales, 1)
         load_rows(wu_s, wu_scales, 2)
         load_rows(wu_s, wu_scales, 3, nc.gpsimd)

from contextlib import ExitStack

import concourse.mybir as mybir
from concourse.masks import make_identity

K, R, N, T, J = 512, 1024, 256, 1024, 512
FLOPS = 2 * K * R * J * 2 + 2 * R * N * J

F32 = mybir.dt.float32
BF16 = mybir.dt.bfloat16
I32 = mybir.dt.int32
U32 = mybir.dt.uint32
U16 = mybir.dt.uint16
U8 = mybir.dt.uint8
FP8X4 = mybir.dt.float8_e4m3fn_x4
FP4X4 = mybir.dt.float4_e2m1fn_x4
RELU = mybir.ActivationFunctionType.Relu
MULT = mybir.AluOpType.mult

P = 128
TOK = 128
TILES = J // TOK
PASS = 512
HALVES = R // PASS


def tile_list_gmlpt_relu_mix_none_kernel(
    tc, tab_words, tab_scales, wg_words, wg_scales, wu_words, wu_scales,
    wd8_words, wd8_scales, wd4_words, wd4_scales, offs, out,
):
    nc = tc.nc
    with ExitStack() as ctx:
        keep = ctx.enter_context(tc.tile_pool(name="keep", bufs=1))
        reuse = ctx.enter_context(tc.tile_pool(name="reuse", bufs=1))
        psum = ctx.enter_context(tc.psum_pool(name="psum", bufs=8))

        def plane(name, width):
            tile = keep.tile([P, width // 4], I32, name=name, align_bytes=64)
            nc.vector.memset(tile[:], 0)
            return tile

        def load_rows(tile, scales, q, queue=nc.sync):
            queue.dma_start(tile[q : P : 32, :], scales[0, q : 16 : 4, :].bitcast(I32))

        offsets = keep.tile([P, J // 16], U16, name="offsets")
        nc.sync.dma_start(offsets[:], offs)
        wg_w = keep.tile([P, 2 * R], U8, name="wg_w", align_bytes=64)
        nc.scalar.dma_start(wg_w[:].bitcast(I32), wg_words[0].bitcast(I32))
        wu_w = keep.tile([P, 2 * R], U8, name="wu_w", align_bytes=64)
        nc.gpsimd.dma_start(wu_w[:].bitcast(I32), wu_words[0].bitcast(I32))

        tab_s = plane("tab_s", T)
        wg_s = plane("wg_s", R)
        wu_s = plane("wu_s", R)
        zeros = keep.tile([P, 2 * P], I32, name="zeros", align_bytes=64)
        nc.vector.memset(zeros[:], 0)
        zero_w = keep.tile([P, P], U32, name="zero_w", align_bytes=64)
        zero_s = keep.tile([P, P], U8, name="zero_s", align_bytes=64)
        nc.vector.quantize_mx(out=zero_w[:].bitcast(FP8X4), scales=zero_s[:], in_=zeros[:].bitcast(BF16))
        wd8_s = plane("wd8_s", N)
        wd4_s = plane("wd4_s", N)
        for q in range(4):
            load_rows(tab_s, tab_scales, q, nc.sync if q % 2 else nc.scalar)
        load_rows(wg_s, wg_scales, 0, nc.scalar)
        tab_w = reuse.tile([P, T], I32, name="tab_w", align_bytes=64, offset=0)
        nc.sync.dma_start(tab_w[:], tab_words[0].rearrange("p t i -> p (t i)").bitcast(I32))
        load_rows(wg_s, wg_scales, 1, nc.scalar)
        load_rows(wg_s, wg_scales, 2, nc.scalar)
        load_rows(wg_s, wg_scales, 3)
        load_rows(wu_s, wu_scales, 0)
        load_rows(wu_s, wu_scales, 1)
        load_rows(wu_s, wu_scales, 2)
        load_rows(wu_s, wu_scales, 3, nc.gpsimd)

        warm_pe = psum.tile([P, PASS], F32, name="warm_pe", tag="bank")
        for i in range(2):
            nc.tensor.matmul_mx(
                out=warm_pe[:], lhsT=zero_w[:].bitcast(FP8X4), lhsT_scale=zero_s[:],
                rhs=wg_w[:, 0 : 2 * PASS].bitcast(FP4X4), rhs_scale=tab_s[:].bitcast(U8)[:, 0:PASS], start=True, stop=True,
            )
        ident = keep.tile([P, P], F32, name="ident", align_bytes=64)
        make_identity(nc, ident[:])
        wd8_w = keep.tile([P, N], I32, name="wd8_w", align_bytes=64)
        nc.sync.dma_start(wd8_w[:], wd8_words[0].rearrange("p n i -> p (n i)").bitcast(I32))
        wd4_w = keep.tile([P, 2 * N], U8, name="wd4_w", align_bytes=64)
        nc.sync.dma_start(wd4_w[:].bitcast(I32), wd4_words[0].bitcast(I32))
        for q in range(4):
            load_rows(wd8_s, wd8_scales, q)
        for q in range(4):
            load_rows(wd4_s, wd4_scales, q)

        v_w, v_s, gate, up, relu, h, ht, hq, codes, cscales = ({} for i in range(10))

        def gather_scales(ts, picked):
            cols = slice(ts[0] * TOK // 16, (ts[-1] + 1) * TOK // 16)
            nc.vector.tensor_copy(picked[:], tab_s[:].bitcast(U8).indirect(offsets[:, cols]))
            for i, t in enumerate(ts):
                v_s[t] = picked[:, TOK * i : TOK * (i + 1)]

        def gather_words(t):
            v_w[t] = keep.tile([P, TOK], U32, name="v_w%d" % t, align_bytes=64)
            nc.vector.tensor_copy(v_w[t][:], tab_w[:].bitcast(U32).indirect(offsets[:, t * TOK // 16 : (t + 1) * TOK // 16]))

        def part(engine, name, source, dtype, tag):
            tile = keep.tile([P, PASS], dtype, name=name, tag=tag, align_bytes=64)
            run = 128 if engine is nc.gpsimd else 8 if dtype == U16 else 16
            (engine.copy if engine is nc.scalar else engine.tensor_copy)(
                tile[:].rearrange("p (i c m) -> p c i m", i=4, m=run),
                source.rearrange("p (c m i) -> p c i m", i=4, m=run),
            )
            return tile[:].bitcast(U8)

        def part_words(engine, name, words, b, tag):
            return part(engine, name, words[:].bitcast(U16)[:, PASS * b : PASS * (b + 1)], U16, tag)

        def part_scales(engine, name, scales, b, tag):
            return part(engine, name, scales[:].bitcast(U8)[:, PASS * b : PASS * (b + 1)], U8, tag)

        def product_lo(t, words, scales):
            acc = psum.tile([P, PASS], F32, name="acc", tag="bank")
            nc.tensor.matmul_mx(
                out=acc[:],
                lhsT=v_w[t][:].bitcast(FP8X4),
                lhsT_scale=v_s[t],
                rhs=words.bitcast(FP4X4),
                rhs_scale=scales[:].bitcast(U8)[:, 0:PASS],
                start=True,
                stop=True,
            )
            return acc[:].rearrange("j (p u e) -> j u p e", u=2, e=2)

        def product_hi(t, words, scales):
            acc = psum.tile([P, 4, TOK], F32, name="acc", tag="bank")
            for i in range(4):
                nc.tensor.matmul_mx(
                    out=acc[:, i, :],
                    lhsT=words[:, 2 * P * i : 2 * P * (i + 1)].bitcast(FP4X4),
                    lhsT_scale=scales[:, P * i : P * (i + 1)],
                    rhs=v_w[t][:].bitcast(FP8X4),
                    rhs_scale=v_s[t],
                    start=True,
                    stop=True,
                )
            return acc[:].rearrange("p i j -> p j i")

        def turned(t, b):
            return b == 0 and t in lo

        def gate_product(t, b):
            gate[t, b] = product_lo(t, wg_w[:, 0 : 2 * PASS], wg_s) if turned(t, b) else product_hi(t, gw[b], gs[b])

        def up_product(t, b):
            up[t, b] = product_lo(t, wu_w[:, 0 : 2 * PASS], wu_s) if turned(t, b) else product_hi(t, uw[b], us[b])

        def rectify(t, b):
            relu[t, b] = keep.tile([P, 2, P, 2] if turned(t, b) else [P, TOK, 4], F32, name="relu%d_%d" % (t, b), tag="relu%d_%d" % (t, b), align_bytes=64)
            nc.scalar.activation(relu[t, b][:], gate[t, b], RELU)

        def multiply(t, b, ts):
            if turned(t, b):
                h[t, b] = keep.tile([P, 2, P, 2], BF16, name="h%d_%d" % (t, b), align_bytes=64)
                dst = h[t, b][:]
            else:
                if (ts, b) not in hq:
                    hq[ts, b] = keep.tile([P, len(ts), TOK, 2], F32, name="hq%d_%d" % (t, b), align_bytes=64)
                dst = hq[ts, b][:, ts.index(t)].bitcast(BF16)
            nc.vector.tensor_tensor(dst, up[t, b], relu[t, b][:], MULT)

        def turn(ts, b):
            acc = psum.tile([P, len(ts), 2, TOK], F32, name="ht", tag="bank")
            for i, t in enumerate(ts):
                words = h[t, b][:].rearrange("j u p e -> j (u p e)").bitcast(F32)
                for u in range(2):
                    nc.tensor.transpose(acc[:, i, u, :], words[:, P * u : P * (u + 1)], ident[:])
            ht[ts, b] = acc

        def interleave(ts, b):
            tile = keep.tile([P, len(ts), TOK, 2], F32, name="hq%d_%d" % (ts[0], b), align_bytes=64)
            nc.scalar.copy(tile[:], ht[ts, b][:].rearrange("p t u j -> p t j u"))
            hq[ts, b] = tile

        def quantise(ts, b):
            c = keep.tile([P, len(ts) * TOK], U32, name="codes%d_%d" % (ts[0], b), align_bytes=64)
            s = keep.tile([P, len(ts) * TOK], U8, name="cscales%d_%d" % (ts[0], b), align_bytes=64)
            nc.vector.quantize_mx(
                out=c[:].bitcast(FP8X4),
                scales=s[:],
                in_=hq[ts, b][:].rearrange("p t j u -> p (t j u)").bitcast(BF16),
            )
            for i, t in enumerate(ts):
                codes[t, b] = c[:, TOK * i : TOK * (i + 1)]
                cscales[t, b] = s[:, TOK * i : TOK * (i + 1)]

        def down_pass(acc, t, b, half, first):
            n0 = P * half
            if b == 0:
                lhs = wd8_w[:, n0 : n0 + P].bitcast(FP8X4)
                lhs_s = wd8_s[:].bitcast(U8)[:, n0 : n0 + P]
            else:
                lhs = wd4_w[:, 2 * n0 : 2 * (n0 + P)].bitcast(FP4X4)
                lhs_s = wd4_s[:].bitcast(U8)[:, n0 : n0 + P]
            nc.tensor.matmul_mx(
                out=acc, lhsT=lhs, lhsT_scale=lhs_s,
                rhs=codes[t, b].bitcast(FP8X4), rhs_scale=cscales[t, b],
                start=(b == first), stop=(b != first),
            )

        out_v = out.rearrange("(h p) j -> p h j", p=P)

        def second_layer(ts):
            y = psum.tile([P, 2, len(ts), TOK], F32, name="y", tag="bank")
            for i, t in enumerate(ts):
                for half in range(2):
                    for b in range(HALVES):
                        down_pass(y[:, half, i, :], t, b, half, 0)
            return y

        def store(ts, y, engine_copy):
            res = keep.tile([P, 2, len(ts) * TOK], F32, name="res%d" % ts[0])
            engine_copy(res[:], y[:].rearrange("p h t j -> p h (t j)"))
            nc.sync.dma_start(out_v[:, :, TOK * ts[0] : TOK * (ts[-1] + 1)], res[:])

        lo, hi = (0, 1), (2, 3)
        gw, uw, gs, us = {}, {}, {}, {}
        gw[1] = part_words(nc.gpsimd, "wg_hi_w", wg_w, 1, "wg_hi_w")
        gw[0] = part_words(nc.gpsimd, "wg_lo_w", wg_w, 0, "wg_lo_w")
        gather_scales(lo, keep.tile([P, 2 * TOK], U8, name="v_s_lo", align_bytes=64))
        for t in range(TILES):
            gather_words(t)
        uw[1] = part_words(nc.scalar, "wu_hi_w", wu_w, 1, "wu_hi_w")
        gather_scales(hi, reuse.tile([P, 2 * TOK], U8, name="v_s_hi", align_bytes=64, offset=0))
        gs[1] = part_scales(nc.gpsimd, "wg_hi_s", wg_s, 1, "wg_hi_s")
        us[1] = part_scales(nc.gpsimd, "wu_hi_s", wu_s, 1, "wu_hi_s")
        gate_product(0, 0)
        up_product(0, 0)
        relu[0, 0] = keep.tile([P, 2, P, 2], F32, name="relu0_0", tag="relu0_0", align_bytes=64)
        h[0, 0] = keep.tile([P, 2, P, 2], BF16, name="h0_0", align_bytes=64)
        for u in range(2):
            nc.scalar.activation(relu[0, 0][:, u], gate[0, 0][:, u], RELU)
            nc.vector.tensor_tensor(h[0, 0][:, u], up[0, 0][:, u], relu[0, 0][:, u], MULT)
        gate_product(1, 0)
        up_product(1, 0)
        rectify(1, 0)
        multiply(1, 0, lo)
        uw[0] = part_words(nc.gpsimd, "wu_lo_w", wu_w, 0, "relu0_0")
        gs[0] = part_scales(nc.gpsimd, "wg_lo_s", wg_s, 0, "relu1_0")
        us[0] = part_scales(nc.gpsimd, "wu_lo_s", wu_s, 0, "wu_lo_s")
        for t in lo:
            gate_product(t, 1)
            up_product(t, 1)
            rectify(t, 1)
            multiply(t, 1, lo)
        for t in hi:
            gate_product(t, 1)
            up_product(t, 1)
            rectify(t, 1)
            multiply(t, 1, hi)
            if t == 2:
                quantise(lo, 1)
        turn(lo, 0)
        interleave(lo, 0)
        quantise(lo, 0)
        for t in hi:
            gate_product(t, 0)
        for t in hi:
            up_product(t, 0)
            rectify(t, 0)
        multiply(2, 0, (2,))
        quantise(hi, 1)
        quantise((2,), 0)
        multiply(3, 0, (3,))
        quantise((3,), 0)
        for t in lo:
            store((t,), second_layer((t,)), nc.scalar.copy)
        y = {}
        for t in hi:
            for half in range(2):
                y[t, half] = psum.tile([P, TOK], F32, name="y%d_%d" % (t, half), tag="bank")
                down_pass(y[t, half][:], t, 1, half, 1)
        for t in hi:
            for half in range(2):
                down_pass(y[t, half][:], t, 0, half, 1)
            for half, copy, queue in ((0, nc.vector.tensor_copy, nc.sync), (1, nc.scalar.copy, nc.scalar)):
                res = keep.tile([P, TOK], F32, name="res%d_%d" % (t, half))
                copy(res[:], y[t, half][:])
                queue.dma_start(out_v[:, half, TOK * t : TOK * (t + 1)], res[:])
